import numpy as np
import ml_dtypes


def mxq(x, axis, fmt="e4m3"):
    dtype, down = {"e4m3": (ml_dtypes.float8_e4m3fn, 7), "e5m2": (ml_dtypes.float8_e5m2, 14)}[fmt]
    v = np.moveaxis(np.asarray(x, np.float32).astype(ml_dtypes.bfloat16).astype(np.float64), axis, -1)
    blocks = v.reshape(v.shape[:-1] + (-1, 32))
    amax = np.abs(blocks).max(-1, keepdims=True)
    byte = np.maximum(np.where(amax > 0, np.frexp(amax)[1] - 1 + 127, 0) - down, 1)
    scale = np.exp2(byte - 127.0)
    codes = (blocks / scale).astype(np.float32).astype(dtype).astype(np.float64)
    return np.moveaxis((codes * scale).reshape(v.shape), -1, axis)


WIDE = False


def mx_kscale(k):
    if not WIDE:
        return np.ones(k)
    levels = np.array([10, -10, 5, -5, 0])
    if k % 512:
        return np.exp2(np.random.permutation(np.resize(levels, k // 32))).repeat(32)
    a = np.empty((k // 512, 16))
    for p in range(k // 512):
        a[p, :8] = np.random.permutation(np.resize(levels, 8))
        for g in range(8):
            far = levels[np.abs(levels - a[p, g]) >= 10]
            a[p, g + 8] = far[np.random.randint(len(far))]
    return np.exp2(a.ravel()).repeat(32)


def f64(x):
    return np.asarray(x).astype(np.float64)


def striped(idx):
    return np.tile(idx.reshape(-1, 16).T, (8, 1)).astype(np.uint16)


def unstriped(offs):
    return offs[:16].T.reshape(-1).astype(np.int64)


def pack_weight(w):
    k, n = w.shape
    w = f64(np.asarray(w, np.float32).astype(ml_dtypes.bfloat16)).reshape(k // 32, 32, n)
    amax = np.abs(w).max(1)
    byte = np.clip(np.where(amax > 0, np.frexp(amax)[1] - 1 + 127 - 7, 1), 1, 254)
    scaled = (w * np.exp2(127.0 - byte)[:, None, :]).reshape(k, n).astype(np.float32)
    words = np.ascontiguousarray(scaled.reshape(k // 512, 128, 4, n).transpose(0, 1, 3, 2)).astype(ml_dtypes.float8_e4m3fn).view(np.uint8)
    return words, np.ascontiguousarray(byte.astype(np.uint8).reshape(k // 512, 16, n))


def unpack_weight(words, scales):
    g, p, n, _ = words.shape
    vals = np.ascontiguousarray(words).view(ml_dtypes.float8_e4m3fn).astype(np.float64) * np.repeat(np.exp2(scales.astype(np.float64) - 127.0), 8, axis=1)[..., None]
    return vals.transpose(0, 1, 3, 2).reshape(g * 512, n)


E2M1 = np.array([0.0, 0.5, 1.0, 1.5, 2.0, 3.0, 4.0, 6.0, -0.0, -0.5, -1.0, -1.5, -2.0, -3.0, -4.0, -6.0])


def pack_fp4(w):
    k, n = w.shape
    w = f64(np.asarray(w, np.float32).astype(ml_dtypes.bfloat16)).reshape(k // 32, 32, n)
    amax = np.abs(w).max(1)
    mant, ex = np.frexp(amax / 6.0)
    byte = np.clip(np.where(amax > 0, np.where(mant > 0.5, ex, ex - 1) + 127, 1), 1, 254)
    scaled = (w * np.exp2(127.0 - byte)[:, None, :]).reshape(k, n).astype(np.float32)
    c = np.ascontiguousarray(scaled.reshape(k // 512, 128, 4, n).transpose(0, 1, 3, 2)).astype(ml_dtypes.float4_e2m1fn).view(np.uint8) & 0xF
    words = (c[..., 0::2] | (c[..., 1::2] << 4)).reshape(k // 512, 128, 2 * n)
    return np.ascontiguousarray(words), np.ascontiguousarray(byte.astype(np.uint8).reshape(k // 512, 16, n))


def unpack_fp4(words, scales):
    g, _, n = scales.shape
    words = np.ascontiguousarray(words).reshape(g, 128, n, 2)
    nib = np.empty((g, 128, n, 4), np.uint8)
    nib[..., 0::2] = words & 0xF
    nib[..., 1::2] = words >> 4
    vals = E2M1[nib] * np.repeat(np.exp2(scales.astype(np.float64) - 127.0), 8, axis=1)[..., None]
    return vals.transpose(0, 1, 3, 2).reshape(g * 512, n)


def sigmoid(v):
    return 1.0 / (1.0 + np.exp(-np.maximum(v, -700.0)))


K, T, S, D, N, H, V, U = 1024, 2048, 512, 2, 256, 512, 256, 512


def setup_inputs():
    n = np.random.standard_normal
    s = mx_kscale(K)[:, None]
    u = mx_kscale(H)
    packed_xT = pack_weight(n((K, T)) * s)
    packed_w1 = pack_fp4(n((K, H)) / np.sqrt(K) / s)
    packed_w2 = pack_fp4(n((K, H)) / np.sqrt(K) / s)
    packed_w3 = pack_fp4(n((H, N)) / np.sqrt(H) / u[:, None])
    return {
        "x_words": packed_xT[0],
        "x_scales": packed_xT[1],
        "w1_words": packed_w1[0],
        "w1_scales": packed_w1[1],
        "w2_words": packed_w2[0],
        "w2_scales": packed_w2[1],
        "st": (n((H, U))).astype(np.float32),
        "lam": (np.random.uniform(0.2, 1.0, (H, U))).astype(np.float32),
        "unit": (np.random.uniform(0.6, 1.4, (H, 1)) * u[:, None]).astype(np.float32),
        "w3_words": packed_w3[0],
        "w3_scales": packed_w3[1],
        "offs": striped(np.random.permutation(T)[:S]),
        "m1": striped(np.random.permutation(np.concatenate([np.arange(V), np.random.randint(0, V, U - V)]))),
        "m2": striped(np.random.randint(0, U, U)),
    }


def reference(x_words, x_scales, w1_words, w1_scales, w2_words, w2_scales, st, lam, unit, w3_words, w3_scales, offs, m1, m2):
    xq = unpack_weight(x_words, x_scales)[:, unstriped(offs)]
    y = unpack_fp4(w1_words, w1_scales).T @ xq
    yg = unpack_fp4(w2_words, w2_scales).T @ xq
    ygt = y * sigmoid(yg)
    lv1 = ygt.reshape(len(ygt), -1, D).sum(axis=2)
    lm = lv1[:, unstriped(m1)]
    lv2 = lm + f64(st)
    lw = lv2 * f64(lam)
    hid = f64(unit) * (np.maximum(lw, lv2[:, unstriped(m2)]))
    return unpack_fp4(w3_words, w3_scales).T @ mxq(hid, 0, "e4m3")

@@ -1,0 +1,233 @@
+from contextlib import ExitStack
+
+import concourse.mybir as mybir
+from concourse.masks import make_identity
+
+K, T, S, H, V, U, N = 1024, 2048, 512, 512, 256, 512, 256
+FLOPS = 2 * (2 * K * H * S + H * N * U)
+
+F32 = mybir.dt.float32
+BF16 = mybir.dt.bfloat16
+I32 = mybir.dt.int32
+U32 = mybir.dt.uint32
+U16 = mybir.dt.uint16
+U8 = mybir.dt.uint8
+FP8X4 = mybir.dt.float8_e4m3fn_x4
+FP4X4 = mybir.dt.float4_e2m1fn_x4
+ALU = mybir.AluOpType
+ACT = mybir.ActivationFunctionType
+
+P = 128
+PACK = 4
+LV1_WINDOW = 544
+LAST_CHUNK = 128
+
+
+def tile_picked_yfenw_max_p_kernel(
+    tc, x_words, x_scales, w1_words, w1_scales, w2_words, w2_scales, st, lam, unit, w3_words, w3_scales, offs, m1, m2, out
+):
+    nc = tc.nc
+    with ExitStack() as ctx:
+        lists = ctx.enter_context(tc.tile_pool(name="lists", bufs=1))
+        keep = ctx.enter_context(tc.tile_pool(name="keep", bufs=1))
+        ring = ctx.enter_context(tc.tile_pool(name="ring", bufs=3))
+        psum = ctx.enter_context(tc.psum_pool(name="psum", bufs=1))
+
+        def held(shape, dtype, name, tag=None):
+            return keep.tile(shape, dtype, name=name, tag=tag or name, align_bytes=64)
+
+        def bank(index, shape, name):
+            return psum.tile(shape, F32, name=name, tag="bank%d" % index)
+
+        xs_window = held([P, T], U8, "xs_window")
+        w2_plane = held([P, 2, H], U8, "w2_plane")
+        w1_plane = held([P, 2, H], U8, "w1_plane")
+        xs1_plane = held([P, S], U8, "xs1_plane")
+        nc.vector.memset(xs_window[:].bitcast(I32), 0)
+        nc.vector.memset(w2_plane[:].rearrange("p o c -> p (o c)").bitcast(I32), 0)
+        nc.vector.memset(w1_plane[:].rearrange("p o c -> p (o c)").bitcast(I32), 0)
+        nc.vector.memset(xs1_plane[:].bitcast(I32), 0)
+
+        def load_weight_scales(queue, plane, scales, q):
+            queue.dma_start(
+                plane[32 * q : 32 * q + 4, :, :].bitcast(I32),
+                scales[:, 4 * q : 4 * q + 4, :].rearrange("o r c -> r o c").bitcast(I32),
+            )
+
+        offs_t = lists.tile([P, S // 16], U16, name="offs_t")
+        m1_t = lists.tile([P, U // 16], U16, name="m1_t")
+        m2_t = lists.tile([P, U // 16], U16, name="m2_t")
+        nc.sync.dma_start(offs_t[:], offs)
+        for r in range(4):
+            nc.sync.dma_start(
+                xs_window[r:P:16, :].bitcast(I32),
+                x_scales.rearrange("o (q r) c -> r q o c", r=4)[r].bitcast(I32),
+            )
+        for q in range(2):
+            load_weight_scales(nc.scalar, w2_plane, w2_scales, q)
+        for q in range(4):
+            load_weight_scales(nc.gpsimd, w1_plane, w1_scales, q)
+        xw = [held([P, T], I32, "xw%d" % o) for o in range(2)]
+        ww = [held([P, 2, 2 * H], U8, "ww%d" % which) for which in range(2)]
+        nc.sync.dma_start(xw[0][:], x_words[0].rearrange("p c r -> p (c r)").bitcast(I32))
+        for q in range(2, 4):
+            load_weight_scales(nc.sync, w2_plane, w2_scales, q)
+        nc.sync.dma_start(ww[1][:].bitcast(I32), w2_words.rearrange("o p c -> p o c").bitcast(I32))
+        nc.sync.dma_start(ww[0][:].bitcast(I32), w1_words.rearrange("o p c -> p o c").bitcast(I32))
+        nc.sync.dma_start(xw[1][:], x_words[1].rearrange("p c r -> p (c r)").bitcast(I32))
+
+        ident = held([P, P], F32, "ident")
+        make_identity(nc, ident[:])
+        lv1 = []
+        for t in range(PACK):
+            lv1.append(held([P, LV1_WINDOW], F32, "lv1_%d" % t))
+            nc.vector.memset(lv1[t][:, V:], 0.0)
+
+        xs_picked = held([P, S], U8, "xs_picked")
+        nc.vector.tensor_copy(xs_picked[:], xs_window[:].indirect(offs_t[:]))
+        xs0_plane = held([P, S], U8, "xs0_plane")
+        nc.vector.tensor_copy(
+            xs0_plane[:].rearrange("p (h d v) -> p h d v", h=2, d=2),
+            xs_picked[:].rearrange("p (h v d) -> p h d v", h=2, d=2),
+        )
+        for q in range(4):
+            nc.sync.dma_start(
+                xs1_plane[32 * q : 32 * q + 4, :].bitcast(I32), xs0_plane[32 * q + 16 : 32 * q + 20, :].bitcast(I32)
+            )
+        xs_plane = [xs0_plane, xs1_plane]
+        nc.sync.dma_start(m1_t[:], m1)
+        st_t = held([P, PACK, U], F32, "st_t")
+        nc.sync.dma_start(st_t[:], st.rearrange("(p t) j -> p t j", t=PACK))
+
+        yg = [bank(b, [P, H], "yg%d" % b) for b in range(4)]
+        y = [bank(4 + b, [P, H], "y%d" % b) for b in range(4)]
+        w_plane = [w1_plane, w2_plane]
+
+        def gather_words(o, h):
+            picked = held([P, 2, P], U32, "xg%d%d" % (o, h))
+            nc.vector.tensor_copy(
+                picked[:].rearrange("p d v -> p v d"),
+                xw[o][:].bitcast(U32).indirect(offs_t[:, 16 * h : 16 * (h + 1)]),
+            )
+            return picked
+
+        def product(acc, which, o, b, picked):
+            nc.tensor.matmul_mx(
+                out=acc[:],
+                lhsT=picked[:, b % 2, :].bitcast(FP8X4),
+                lhsT_scale=xs_plane[o][:, P * b : P * (b + 1)],
+                rhs=ww[which][:, o, :].bitcast(FP4X4),
+                rhs_scale=w_plane[which][:, o, :],
+                start=(o == 0),
+                stop=(o == 1),
+            )
+
+        picked0 = [gather_words(0, h) for h in range(2)]
+        nc.sync.dma_start(m2_t[:], m2)
+        lam_t = held([P, PACK, U], F32, "lam_t")
+        nc.sync.dma_start(lam_t[:], lam.rearrange("(p t) j -> p t j", t=PACK))
+        for b in range(4):
+            product(yg[b], 1, 0, b, picked0[b // 2])
+        for b in range(4):
+            product(y[b], 0, 0, b, picked0[b // 2])
+        for h in range(2):
+            picked1 = gather_words(1, h)
+            for b in (2 * h, 2 * h + 1):
+                product(yg[b], 1, 1, b, picked1)
+            for b in (2 * h, 2 * h + 1):
+                product(y[b], 0, 1, b, picked1)
+
+        unit_t = held([P, PACK], F32, "unit_t")
+        nc.sync.dma_start(unit_t[:], unit.rearrange("(p t) one -> p (t one)", t=PACK))
+        w3w = held([P, 2 * N], U8, "w3w")
+        w3_plane = held([P, N], U8, "w3_plane")
+        nc.vector.memset(w3_plane[:].bitcast(I32), 0)
+        nc.sync.dma_start(w3w[:].bitcast(I32), w3_words[0].bitcast(I32))
+        for q in range(4):
+            nc.sync.dma_start(
+                w3_plane[32 * q : 32 * q + 4, :].bitcast(I32), w3_scales[0, 4 * q : 4 * q + 4, :].bitcast(I32)
+            )
+
+        gated = {}
+        for h in range(2):
+            for u in range(2):
+                for b in (2 * h, 2 * h + 1):
+                    sig = ring.tile([P, P, 2], F32, name="sig")
+                    nc.scalar.activation(
+                        sig[:], yg[b][:].rearrange("p (m t) -> p m t", t=PACK)[:, :, 2 * u : 2 * u + 2], ACT.Sigmoid
+                    )
+                    gated[b, u] = held([P, 2, P], F32, "gated%d%d" % (b, u))
+                    nc.vector.tensor_tensor(
+                        gated[b, u][:].rearrange("p e m -> p m e"),
+                        y[b][:].rearrange("p (m t) -> p m t", t=PACK)[:, :, 2 * u : 2 * u + 2],
+                        sig[:],
+                        ALU.mult,
+                    )
+        for t in range(PACK):
+            turned = bank((0, 1, 4, 5)[t], [P, V], "turned%d" % t)
+            for h in range(2):
+                for d in range(2):
+                    nc.tensor.matmul(
+                        turned[:, P * h : P * (h + 1)],
+                        gated[2 * h + d, t // 2][:, t % 2, :],
+                        ident[:],
+                        is_transpose=True,
+                        start=(d == 0),
+                        stop=(d == 1),
+                    )
+            nc.scalar.copy(lv1[t][:, :V], turned[:])
+
+        hid = [held([P, LAST_CHUNK, PACK], BF16, "hid%d" % c) for c in range(U // LAST_CHUNK)]
+        lv2, lw = [], []
+
+        def level_two(t):
+            lv2.append(held([P, U], F32, "lv2_%d" % t))
+            nc.vector.tensor_tensor(lv2[t][:], lv1[t][:].indirect(m1_t[:]), st_t[:, t, :], ALU.add)
+            lw.append(held([P, U], F32, "lw_%d" % t))
+            nc.vector.tensor_tensor(lw[t][:], lv2[t][:], lam_t[:, t, :], ALU.mult)
+
+        def read_other(t, j0, width):
+            other = ring.tile([P, width], F32, name="other%d" % width)
+            nc.vector.tensor_copy(other[:], lv2[t][:].indirect(m2_t[:, j0 // 16 : (j0 + width) // 16]))
+            larger = ring.tile([P, width], F32, name="larger%d" % width)
+            nc.vector.tensor_tensor(larger[:], other[:], lw[t][:, j0 : j0 + width], ALU.max)
+            for c in range(j0 // LAST_CHUNK, (j0 + width) // LAST_CHUNK):
+                nc.scalar.activation(
+                    hid[c][:, :, t],
+                    larger[:, c * LAST_CHUNK - j0 : (c + 1) * LAST_CHUNK - j0],
+                    ACT.Copy,
+                    scale=unit_t[:, t : t + 1],
+                )
+
+        def project(c):
+            codes = held([P, LAST_CHUNK], U32, "codes%d" % c)
+            plane = held([P, LAST_CHUNK], U8, "plane%d" % c)
+            nc.vector.quantize_mx(
+                out=codes[:].bitcast(FP8X4), scales=plane[:], in_=hid[c][:].rearrange("p j t -> p (j t)")
+            )
+            acc = bank((2, 3, 6, 7)[c], [P, 2, LAST_CHUNK], "acc%d" % c)
+            for a in range(2):
+                nc.tensor.matmul_mx(
+                    out=acc[:, a, :],
+                    lhsT=w3w[:, 2 * P * a : 2 * P * (a + 1)].bitcast(FP4X4),
+                    lhsT_scale=w3_plane[:, P * a : P * (a + 1)],
+                    rhs=codes[:].bitcast(FP8X4),
+                    rhs_scale=plane[:],
+                    start=True,
+                    stop=True,
+                )
+            result = held([P, 2, LAST_CHUNK], F32, "result%d" % c)
+            nc.vector.tensor_copy(result[:], acc[:])
+            nc.sync.dma_start(
+                out.rearrange("(a p) j -> p a j", p=P)[:, :, c * LAST_CHUNK : (c + 1) * LAST_CHUNK], result[:]
+            )
+
+        level_two(0)
+        for t in range(PACK - 1):
+            level_two(t + 1)
+            for h in range(2):
+                read_other(t, 256 * h, 256)
+        for c in range(U // LAST_CHUNK):
+            read_other(PACK - 1, c * LAST_CHUNK, LAST_CHUNK)
+        for c in range(U // LAST_CHUNK):
+            project(c)

@@ -19,7 +19,7 @@ ACT = mybir.ActivationFunctionType
 
 P = 128
 PACK = 4
-LV1_WINDOW = 544
+LV1_WINDOW = 272
 LAST_CHUNK = 128
 
 
@@ -30,7 +30,7 @@ def tile_picked_yfenw_max_p_kernel(
     with ExitStack() as ctx:
         lists = ctx.enter_context(tc.tile_pool(name="lists", bufs=1))
         keep = ctx.enter_context(tc.tile_pool(name="keep", bufs=1))
-        ring = ctx.enter_context(tc.tile_pool(name="ring", bufs=3))
+        ring = ctx.enter_context(tc.tile_pool(name="ring", bufs=8))
         psum = ctx.enter_context(tc.psum_pool(name="psum", bufs=1))
 
         def held(shape, dtype, name, tag=None):
@@ -43,9 +43,16 @@ def tile_picked_yfenw_max_p_kernel(
         w2_plane = held([P, 2, H], U8, "w2_plane")
         w1_plane = held([P, 2, H], U8, "w1_plane")
         xs1_plane = held([P, S], U8, "xs1_plane")
+        lv1 = [held([P, LV1_WINDOW], F32, "lv1_%d" % t) for t in range(PACK)]
+        zeros = [held([P, LV1_WINDOW - V], F32, "zeros%d" % t, tag) for t, tag in enumerate(("xw0", "ww1", "ww0", "xw1"))]
+        nc.gpsimd.memset(w1_plane[:].rearrange("p o c -> p (o c)").bitcast(I32), 0)
+        for t in range(PACK):
+            nc.vector.memset(zeros[t][:], 0.0)
         nc.vector.memset(xs_window[:].bitcast(I32), 0)
+        nc.vector.tensor_copy(lv1[0][:, V:], zeros[0][:])
         nc.vector.memset(w2_plane[:].rearrange("p o c -> p (o c)").bitcast(I32), 0)
-        nc.vector.memset(w1_plane[:].rearrange("p o c -> p (o c)").bitcast(I32), 0)
+        for t in range(1, PACK):
+            nc.vector.tensor_copy(lv1[t][:, V:], zeros[t][:])
         nc.vector.memset(xs1_plane[:].bitcast(I32), 0)
 
         def load_weight_scales(queue, plane, scales, q):
@@ -58,19 +65,19 @@ def tile_picked_yfenw_max_p_kernel(
         m1_t = lists.tile([P, U // 16], U16, name="m1_t")
         m2_t = lists.tile([P, U // 16], U16, name="m2_t")
         nc.sync.dma_start(offs_t[:], offs)
+        nc.sync.dma_start(m1_t[:], m1)
+        nc.sync.dma_start(m2_t[:], m2)
         for r in range(4):
             nc.sync.dma_start(
                 xs_window[r:P:16, :].bitcast(I32),
                 x_scales.rearrange("o (q r) c -> r q o c", r=4)[r].bitcast(I32),
             )
-        for q in range(2):
-            load_weight_scales(nc.scalar, w2_plane, w2_scales, q)
         for q in range(4):
             load_weight_scales(nc.gpsimd, w1_plane, w1_scales, q)
         xw = [held([P, T], I32, "xw%d" % o) for o in range(2)]
         ww = [held([P, 2, 2 * H], U8, "ww%d" % which) for which in range(2)]
         nc.sync.dma_start(xw[0][:], x_words[0].rearrange("p c r -> p (c r)").bitcast(I32))
-        for q in range(2, 4):
+        for q in range(4):
             load_weight_scales(nc.sync, w2_plane, w2_scales, q)
         nc.sync.dma_start(ww[1][:].bitcast(I32), w2_words.rearrange("o p c -> p o c").bitcast(I32))
         nc.sync.dma_start(ww[0][:].bitcast(I32), w1_words.rearrange("o p c -> p o c").bitcast(I32))
@@ -78,12 +85,8 @@ def tile_picked_yfenw_max_p_kernel(
 
         ident = held([P, P], F32, "ident")
         make_identity(nc, ident[:])
-        lv1 = []
-        for t in range(PACK):
-            lv1.append(held([P, LV1_WINDOW], F32, "lv1_%d" % t))
-            nc.vector.memset(lv1[t][:, V:], 0.0)
 
-        xs_picked = held([P, S], U8, "xs_picked")
+        xs_picked = held([P, S], U8, "xs_picked", "then_st")
         nc.vector.tensor_copy(xs_picked[:], xs_window[:].indirect(offs_t[:]))
         xs0_plane = held([P, S], U8, "xs0_plane")
         nc.vector.tensor_copy(
@@ -95,9 +98,13 @@ def tile_picked_yfenw_max_p_kernel(
                 xs1_plane[32 * q : 32 * q + 4, :].bitcast(I32), xs0_plane[32 * q + 16 : 32 * q + 20, :].bitcast(I32)
             )
         xs_plane = [xs0_plane, xs1_plane]
-        nc.sync.dma_start(m1_t[:], m1)
-        st_t = held([P, PACK, U], F32, "st_t")
-        nc.sync.dma_start(st_t[:], st.rearrange("(p t) j -> p t j", t=PACK))
+        st_rows = st.rearrange("(p t) j -> p t j", t=PACK)
+        st_first = held([P, U + PACK], F32, "st_first", "then_st")
+        unit_t = st_first[:, U:]
+        nc.sync.dma_start(unit_t, unit.rearrange("(p t) one -> p (t one)", t=PACK))
+        nc.sync.dma_start(st_first[:, :U], st_rows[:, 0, :])
+        st_rest = held([P, PACK - 1, U], F32, "st_rest", "xw0")
+        st_sized = [held([P, U], F32, "st_sized%d" % t) for t in range(PACK)]
 
         yg = [bank(b, [P, H], "yg%d" % b) for b in range(4)]
         y = [bank(4 + b, [P, H], "y%d" % b) for b in range(4)]
@@ -123,24 +130,27 @@ def tile_picked_yfenw_max_p_kernel(
             )
 
         picked0 = [gather_words(0, h) for h in range(2)]
-        nc.sync.dma_start(m2_t[:], m2)
-        lam_t = held([P, PACK, U], F32, "lam_t")
-        nc.sync.dma_start(lam_t[:], lam.rearrange("(p t) j -> p t j", t=PACK))
+        nc.sync.dma_start(st_rest[:], st_rows[:, 1:, :])
+        picked1 = [gather_words(1, h) for h in range(2)]
+        picked = [picked0, picked1]
+        for o in range(2):
+            for b in range(4):
+                product(yg[b], 1, o, b, picked[o][b // 2])
         for b in range(4):
-            product(yg[b], 1, 0, b, picked0[b // 2])
-        for b in range(4):
-            product(y[b], 0, 0, b, picked0[b // 2])
-        for h in range(2):
-            picked1 = gather_words(1, h)
-            for b in (2 * h, 2 * h + 1):
-                product(yg[b], 1, 1, b, picked1)
-            for b in (2 * h, 2 * h + 1):
-                product(y[b], 0, 1, b, picked1)
-
-        unit_t = held([P, PACK], F32, "unit_t")
-        nc.sync.dma_start(unit_t[:], unit.rearrange("(p t) one -> p (t one)", t=PACK))
-        w3w = held([P, 2 * N], U8, "w3w")
-        w3_plane = held([P, N], U8, "w3_plane")
+            for o in range(2):
+                product(y[b], 0, o, b, picked[o][b // 2])
+        late = held([P, PACK * U + 24], F32, "late", "xw1")
+        lam_t = late[:, : PACK * U].rearrange("p (t j) -> p t j", t=PACK)
+        size = late[:, PACK * U : PACK * U + PACK]
+        is_plus = late[:, PACK * U + 8 : PACK * U + 8 + PACK]
+        sign = late[:, PACK * U + 16 : PACK * U + 16 + PACK]
+        nc.vector.scalar_tensor_tensor(size, unit_t, -1.0, unit_t, ALU.mult, ALU.max)
+        nc.vector.tensor_scalar(is_plus, unit_t, 0.0, 2.0, ALU.is_ge, ALU.mult)
+        nc.vector.tensor_scalar(sign, is_plus, -1.0, None, ALU.add)
+        nc.vector.tensor_scalar(st_sized[0][:], st_first[:, :U], size[:, 0:1], None, ALU.mult)
+        nc.sync.dma_start(late[:, : PACK * U], lam.rearrange("(p t) j -> p (t j)", t=PACK))
+        w3w = held([P, 2 * N], U8, "w3w", "xg00")
+        w3_plane = held([P, N], U8, "w3_plane", "xg01")
         nc.vector.memset(w3_plane[:].bitcast(I32), 0)
         nc.sync.dma_start(w3w[:].bitcast(I32), w3_words[0].bitcast(I32))
         for q in range(4):
@@ -149,8 +159,8 @@ def tile_picked_yfenw_max_p_kernel(
             )
 
         gated = {}
-        for h in range(2):
-            for u in range(2):
+        for u in range(2):
+            for h in range(2):
                 for b in (2 * h, 2 * h + 1):
                     sig = ring.tile([P, P, 2], F32, name="sig")
                     nc.scalar.activation(
@@ -175,28 +185,36 @@ def tile_picked_yfenw_max_p_kernel(
                         start=(d == 0),
                         stop=(d == 1),
                     )
-            nc.scalar.copy(lv1[t][:, :V], turned[:])
+            nc.scalar.activation(lv1[t][:, :V], turned[:], ACT.Copy, scale=size[:, t : t + 1])
+            if t > 0:
+                nc.scalar.activation(st_sized[t][:], st_rest[:, t - 1, :], ACT.Copy, scale=size[:, t : t + 1])
 
         hid = [held([P, LAST_CHUNK, PACK], BF16, "hid%d" % c) for c in range(U // LAST_CHUNK)]
         lv2, lw = [], []
 
         def level_two(t):
             lv2.append(held([P, U], F32, "lv2_%d" % t))
-            nc.vector.tensor_tensor(lv2[t][:], lv1[t][:].indirect(m1_t[:]), st_t[:, t, :], ALU.add)
-            lw.append(held([P, U], F32, "lw_%d" % t))
+            for h in range(2):
+                nc.vector.tensor_tensor(
+                    lv2[t][:, 256 * h : 256 * (h + 1)],
+                    lv1[t][:].indirect(m1_t[:, 16 * h : 16 * (h + 1)]),
+                    st_sized[t][:, 256 * h : 256 * (h + 1)],
+                    ALU.add,
+                )
+            lw.append(held([P, U], BF16, "lw_%d" % t))
             nc.vector.tensor_tensor(lw[t][:], lv2[t][:], lam_t[:, t, :], ALU.mult)
 
         def read_other(t, j0, width):
-            other = ring.tile([P, width], F32, name="other%d" % width)
+            other = ring.tile([P, width], BF16, name="other%d" % width)
             nc.vector.tensor_copy(other[:], lv2[t][:].indirect(m2_t[:, j0 // 16 : (j0 + width) // 16]))
-            larger = ring.tile([P, width], F32, name="larger%d" % width)
+            larger = ring.tile([P, width], BF16, name="larger%d" % width)
             nc.vector.tensor_tensor(larger[:], other[:], lw[t][:, j0 : j0 + width], ALU.max)
             for c in range(j0 // LAST_CHUNK, (j0 + width) // LAST_CHUNK):
                 nc.scalar.activation(
                     hid[c][:, :, t],
                     larger[:, c * LAST_CHUNK - j0 : (c + 1) * LAST_CHUNK - j0],
                     ACT.Copy,
-                    scale=unit_t[:, t : t + 1],
+                    scale=sign[:, t : t + 1],
                 )
 
         def project(c):

@@ -1,7 +1,6 @@
 from contextlib import ExitStack
 
 import concourse.mybir as mybir
-from concourse.masks import make_identity
 
 K, T, S, H, V, U, N = 1024, 2048, 512, 512, 256, 512, 256
 FLOPS = 2 * (2 * K * H * S + H * N * U)
@@ -18,9 +17,13 @@ ALU = mybir.AluOpType
 ACT = mybir.ActivationFunctionType
 
 P = 128
-PACK = 4
-LV1_WINDOW = 272
-LAST_CHUNK = 128
+SLOTS = 4
+PASSES = K // (P * SLOTS)
+QUADRANTS = 4
+HALF = 256
+SPARE = 16
+CHUNK = 128
+CHUNKS = U // CHUNK
 
 
 def tile_picked_yfenw_max_p_kernel(
@@ -30,222 +33,198 @@ def tile_picked_yfenw_max_p_kernel(
     with ExitStack() as ctx:
         lists = ctx.enter_context(tc.tile_pool(name="lists", bufs=1))
         keep = ctx.enter_context(tc.tile_pool(name="keep", bufs=1))
-        ring = ctx.enter_context(tc.tile_pool(name="ring", bufs=8))
         psum = ctx.enter_context(tc.psum_pool(name="psum", bufs=1))
 
-        def held(shape, dtype, name, tag=None):
-            return keep.tile(shape, dtype, name=name, tag=tag or name, align_bytes=64)
+        def held(shape, dtype, name, after=None):
+            return keep.tile(shape, dtype, name=name, tag=after or name, align_bytes=64)
 
         def bank(index, shape, name):
             return psum.tile(shape, F32, name=name, tag="bank%d" % index)
 
-        xs_window = held([P, T], U8, "xs_window")
-        w2_plane = held([P, 2, H], U8, "w2_plane")
-        w1_plane = held([P, 2, H], U8, "w1_plane")
-        xs1_plane = held([P, S], U8, "xs1_plane")
-        lv1 = [held([P, LV1_WINDOW], F32, "lv1_%d" % t) for t in range(PACK)]
-        zeros = [held([P, LV1_WINDOW - V], F32, "zeros%d" % t, tag) for t, tag in enumerate(("xw0", "ww1", "ww0", "xw1"))]
-        nc.gpsimd.memset(w1_plane[:].rearrange("p o c -> p (o c)").bitcast(I32), 0)
-        for t in range(PACK):
-            nc.vector.memset(zeros[t][:], 0.0)
-        nc.vector.memset(xs_window[:].bitcast(I32), 0)
-        nc.vector.tensor_copy(lv1[0][:, V:], zeros[0][:])
-        nc.vector.memset(w2_plane[:].rearrange("p o c -> p (o c)").bitcast(I32), 0)
-        for t in range(1, PACK):
-            nc.vector.tensor_copy(lv1[t][:, V:], zeros[t][:])
-        nc.vector.memset(xs1_plane[:].bitcast(I32), 0)
+        def entries(offsets, first, count):
+            return offsets[:, first // 16 : (first + count) // 16]
 
-        def load_weight_scales(queue, plane, scales, q):
+        xs_window = held([P, T], U8, "xs_window")
+        xs1 = held([P, S], U8, "xs1")
+        ws_loaded = [held([P, PASSES, H], U8, "ws_loaded%d" % g) for g in range(2)]
+        lv1 = [held([P, V + SPARE], F32, "lv1_%d" % t) for t in range(SLOTS)]
+        zeros = [held([P, SPARE], F32, "xw%d" % o) for o in range(PASSES)]
+        for o in range(PASSES):
+            nc.vector.memset(zeros[o][:], 0.0)
+        nc.vector.memset(xs_window[:, : T // 2].bitcast(I32), 0)
+        nc.gpsimd.memset(xs_window[:, T // 2 :].bitcast(I32), 0)
+        nc.gpsimd.memset(ws_loaded[0][:].rearrange("p o c -> p (o c)").bitcast(I32), 0)
+        nc.vector.memset(ws_loaded[1][:].rearrange("p o c -> p (o c)").bitcast(I32), 0)
+        for t in range(SLOTS):
+            nc.vector.tensor_copy(lv1[t][:, V:], zeros[t // 2][:])
+        nc.vector.memset(xs1[:].bitcast(I32), 0)
+
+        def load_weight_scales(queue, g, q):
             queue.dma_start(
-                plane[32 * q : 32 * q + 4, :, :].bitcast(I32),
-                scales[:, 4 * q : 4 * q + 4, :].rearrange("o r c -> r o c").bitcast(I32),
+                ws_loaded[g][32 * q : 32 * q + 4, :, :].bitcast(I32),
+                (w1_scales, w2_scales)[g][:, 4 * q : 4 * q + 4, :].rearrange("o r c -> r o c").bitcast(I32),
             )
 
         offs_t = lists.tile([P, S // 16], U16, name="offs_t")
         m1_t = lists.tile([P, U // 16], U16, name="m1_t")
         m2_t = lists.tile([P, U // 16], U16, name="m2_t")
+        xw = [held([P, T], I32, "xw_table%d" % o, after="xw%d" % o) for o in range(PASSES)]
+        ww_loaded = [held([P, PASSES, 2 * H], U8, "ww_loaded%d" % g) for g in range(2)]
         nc.sync.dma_start(offs_t[:], offs)
-        nc.sync.dma_start(m1_t[:], m1)
-        nc.sync.dma_start(m2_t[:], m2)
+        nc.sync.dma_start(ww_loaded[1][:].bitcast(I32), w2_words.rearrange("o p c -> p o c").bitcast(I32))
+        nc.sync.dma_start(ww_loaded[0][:].bitcast(I32), w1_words.rearrange("o p c -> p o c").bitcast(I32))
         for r in range(4):
             nc.sync.dma_start(
                 xs_window[r:P:16, :].bitcast(I32),
                 x_scales.rearrange("o (q r) c -> r q o c", r=4)[r].bitcast(I32),
             )
-        for q in range(4):
-            load_weight_scales(nc.gpsimd, w1_plane, w1_scales, q)
-        xw = [held([P, T], I32, "xw%d" % o) for o in range(2)]
-        ww = [held([P, 2, 2 * H], U8, "ww%d" % which) for which in range(2)]
         nc.sync.dma_start(xw[0][:], x_words[0].rearrange("p c r -> p (c r)").bitcast(I32))
-        for q in range(4):
-            load_weight_scales(nc.sync, w2_plane, w2_scales, q)
-        nc.sync.dma_start(ww[1][:].bitcast(I32), w2_words.rearrange("o p c -> p o c").bitcast(I32))
-        nc.sync.dma_start(ww[0][:].bitcast(I32), w1_words.rearrange("o p c -> p o c").bitcast(I32))
+        for q in range(QUADRANTS):
+            load_weight_scales(nc.sync, 1, q)
+        for q in range(QUADRANTS):
+            load_weight_scales(nc.gpsimd if q < 2 else nc.sync, 0, q)
         nc.sync.dma_start(xw[1][:], x_words[1].rearrange("p c r -> p (c r)").bitcast(I32))
+        nc.sync.dma_start(m1_t[:], m1)
+        nc.sync.dma_start(m2_t[:], m2)
 
-        ident = held([P, P], F32, "ident")
-        make_identity(nc, ident[:])
-
-        xs_picked = held([P, S], U8, "xs_picked", "then_st")
-        nc.vector.tensor_copy(xs_picked[:], xs_window[:].indirect(offs_t[:]))
-        xs0_plane = held([P, S], U8, "xs0_plane")
-        nc.vector.tensor_copy(
-            xs0_plane[:].rearrange("p (h d v) -> p h d v", h=2, d=2),
-            xs_picked[:].rearrange("p (h v d) -> p h d v", h=2, d=2),
-        )
-        for q in range(4):
-            nc.sync.dma_start(
-                xs1_plane[32 * q : 32 * q + 4, :].bitcast(I32), xs0_plane[32 * q + 16 : 32 * q + 20, :].bitcast(I32)
-            )
-        xs_plane = [xs0_plane, xs1_plane]
-        st_rows = st.rearrange("(p t) j -> p t j", t=PACK)
-        st_first = held([P, U + PACK], F32, "st_first", "then_st")
+        xs0 = held([P, S], U8, "xs0")
+        nc.vector.tensor_copy(xs0[:], xs_window[:].indirect(offs_t[:]))
+        for q in range(QUADRANTS):
+            nc.sync.dma_start(xs1[32 * q : 32 * q + 4, :].bitcast(I32), xs0[32 * q + 16 : 32 * q + 20, :].bitcast(I32))
+        xs = [xs0, xs1]
+        st_rows = st.rearrange("(p t) j -> p t j", t=SLOTS)
+        st_first = held([P, U + SLOTS], F32, "st_first", after="xs_window")
         unit_t = st_first[:, U:]
-        nc.sync.dma_start(unit_t, unit.rearrange("(p t) one -> p (t one)", t=PACK))
+        nc.sync.dma_start(unit_t, unit.rearrange("(p t) one -> p (t one)", t=SLOTS))
         nc.sync.dma_start(st_first[:, :U], st_rows[:, 0, :])
-        st_rest = held([P, PACK - 1, U], F32, "st_rest", "xw0")
-        st_sized = [held([P, U], F32, "st_sized%d" % t) for t in range(PACK)]
 
-        yg = [bank(b, [P, H], "yg%d" % b) for b in range(4)]
-        y = [bank(4 + b, [P, H], "y%d" % b) for b in range(4)]
-        w_plane = [w1_plane, w2_plane]
-
-        def gather_words(o, h):
-            picked = held([P, 2, P], U32, "xg%d%d" % (o, h))
-            nc.vector.tensor_copy(
-                picked[:].rearrange("p d v -> p v d"),
-                xw[o][:].bitcast(U32).indirect(offs_t[:, 16 * h : 16 * (h + 1)]),
-            )
-            return picked
-
-        def product(acc, which, o, b, picked):
-            nc.tensor.matmul_mx(
-                out=acc[:],
-                lhsT=picked[:, b % 2, :].bitcast(FP8X4),
-                lhsT_scale=xs_plane[o][:, P * b : P * (b + 1)],
-                rhs=ww[which][:, o, :].bitcast(FP4X4),
-                rhs_scale=w_plane[which][:, o, :],
-                start=(o == 0),
-                stop=(o == 1),
-            )
-
-        picked0 = [gather_words(0, h) for h in range(2)]
+        picked = [held([P, S], U32, "picked%d" % o) for o in range(PASSES)]
+        for o in range(PASSES):
+            nc.vector.tensor_copy(picked[o][:], xw[o][:].bitcast(U32).indirect(offs_t[:]))
+        st_rest = held([P, SLOTS - 1, U], F32, "st_rest", after="xw0")
         nc.sync.dma_start(st_rest[:], st_rows[:, 1:, :])
-        picked1 = [gather_words(1, h) for h in range(2)]
-        picked = [picked0, picked1]
-        for o in range(2):
-            for b in range(4):
-                product(yg[b], 1, o, b, picked[o][b // 2])
-        for b in range(4):
-            for o in range(2):
-                product(y[b], 0, o, b, picked[o][b // 2])
-        late = held([P, PACK * U + 24], F32, "late", "xw1")
-        lam_t = late[:, : PACK * U].rearrange("p (t j) -> p t j", t=PACK)
-        size = late[:, PACK * U : PACK * U + PACK]
-        is_plus = late[:, PACK * U + 8 : PACK * U + 8 + PACK]
-        sign = late[:, PACK * U + 16 : PACK * U + 16 + PACK]
-        nc.vector.scalar_tensor_tensor(size, unit_t, -1.0, unit_t, ALU.mult, ALU.max)
-        nc.vector.tensor_scalar(is_plus, unit_t, 0.0, 2.0, ALU.is_ge, ALU.mult)
-        nc.vector.tensor_scalar(sign, is_plus, -1.0, None, ALU.add)
-        nc.vector.tensor_scalar(st_sized[0][:], st_first[:, :U], size[:, 0:1], None, ALU.mult)
-        nc.sync.dma_start(late[:, : PACK * U], lam.rearrange("(p t) j -> p (t j)", t=PACK))
-        w3w = held([P, 2 * N], U8, "w3w", "xg00")
-        w3_plane = held([P, N], U8, "w3_plane", "xg01")
-        nc.vector.memset(w3_plane[:].bitcast(I32), 0)
-        nc.sync.dma_start(w3w[:].bitcast(I32), w3_words[0].bitcast(I32))
-        for q in range(4):
-            nc.sync.dma_start(
-                w3_plane[32 * q : 32 * q + 4, :].bitcast(I32), w3_scales[0, 4 * q : 4 * q + 4, :].bitcast(I32)
-            )
 
-        gated = {}
-        for u in range(2):
+        ww, ws = {}, {}
+        for o in range(PASSES):
+            for g in (1, 0):
+                ww[g, o] = held([P, SLOTS, P, 2], U8, "ww%d%d" % (g, o))
+                ws[g, o] = held([P, SLOTS, P], U8, "ws%d%d" % (g, o))
+                nc.vector.tensor_copy(ws[g, o][:], ws_loaded[g][:, o, :].rearrange("p (m t) -> p t m", t=SLOTS))
+                nc.vector.tensor_copy(ww[g, o][:], ww_loaded[g][:, o, :].rearrange("p (m t b) -> p t m b", t=SLOTS, b=2))
+
+        late = held([P, SLOTS * U + 24], F32, "late", after="xw1")
+        lam_t = late[:, : SLOTS * U].rearrange("p (t j) -> p t j", t=SLOTS)
+        size = late[:, SLOTS * U : SLOTS * U + SLOTS]
+        twice_plus = late[:, SLOTS * U + 8 : SLOTS * U + 8 + SLOTS]
+        sign = late[:, SLOTS * U + 16 : SLOTS * U + 16 + SLOTS]
+        st_sized = [held([P, U], F32, "st_sized%d" % t) for t in range(SLOTS)]
+        nc.vector.scalar_tensor_tensor(size, unit_t, -1.0, unit_t, ALU.mult, ALU.max)
+        nc.vector.tensor_scalar(twice_plus, unit_t, 0.0, 2.0, ALU.is_ge, ALU.mult)
+        nc.vector.tensor_scalar(st_sized[0][:], st_first[:, :U], size[:, 0:1], None, ALU.mult)
+        nc.vector.tensor_scalar(sign, twice_plus, -1.0, None, ALU.add)
+        nc.sync.dma_start(late[:, : SLOTS * U], lam.rearrange("(p t) j -> p (t j)", t=SLOTS))
+        w3w = held([P, 2 * N], U8, "w3w", after="ws_loaded1")
+        w3s = held([P, N], U8, "w3s", after="ws_loaded0")
+        nc.vector.memset(w3s[:].bitcast(I32), 0)
+        nc.sync.dma_start(w3w[:].bitcast(I32), w3_words[0].bitcast(I32))
+        for q in range(QUADRANTS):
+            nc.sync.dma_start(w3s[32 * q : 32 * q + 4, :].bitcast(I32), w3_scales[0, 4 * q : 4 * q + 4, :].bitcast(I32))
+
+        sums = {}
+
+        def products(t):
+            for g in (1, 0):
+                sums[g, t] = bank(2 * (t % 2) + g, [P, S], "sums%d%d" % (g, t))
+                for o in range(PASSES):
+                    nc.tensor.matmul_mx(
+                        out=sums[g, t][:],
+                        lhsT=ww[g, o][:, t, :, :].rearrange("p m b -> p (m b)").bitcast(FP4X4),
+                        lhsT_scale=ws[g, o][:, t, :],
+                        rhs=picked[o][:].bitcast(FP8X4),
+                        rhs_scale=xs[o][:],
+                        start=(o == 0),
+                        stop=(o == PASSES - 1),
+                    )
+
+        hid = [held([P, CHUNK, SLOTS], BF16, "hid%d" % c) for c in range(CHUNKS)]
+        lv2, lw = {}, {}
+
+        def level_one(t):
+            products(t)
+            gated = held([P, 2, V], F32, "gated%d" % t)
             for h in range(2):
-                for b in (2 * h, 2 * h + 1):
-                    sig = ring.tile([P, P, 2], F32, name="sig")
-                    nc.scalar.activation(
-                        sig[:], yg[b][:].rearrange("p (m t) -> p m t", t=PACK)[:, :, 2 * u : 2 * u + 2], ACT.Sigmoid
-                    )
-                    gated[b, u] = held([P, 2, P], F32, "gated%d%d" % (b, u))
-                    nc.vector.tensor_tensor(
-                        gated[b, u][:].rearrange("p e m -> p m e"),
-                        y[b][:].rearrange("p (m t) -> p m t", t=PACK)[:, :, 2 * u : 2 * u + 2],
-                        sig[:],
-                        ALU.mult,
-                    )
-        for t in range(PACK):
-            turned = bank((0, 1, 4, 5)[t], [P, V], "turned%d" % t)
-            for h in range(2):
-                for d in range(2):
-                    nc.tensor.matmul(
-                        turned[:, P * h : P * (h + 1)],
-                        gated[2 * h + d, t // 2][:, t % 2, :],
-                        ident[:],
-                        is_transpose=True,
-                        start=(d == 0),
-                        stop=(d == 1),
-                    )
-            nc.scalar.activation(lv1[t][:, :V], turned[:], ACT.Copy, scale=size[:, t : t + 1])
+                tokens = slice(HALF * h, HALF * (h + 1))
+                sig = held([P, HALF], F32, "sig%d%d" % (t, h))
+                nc.scalar.activation(sig[:], sums[1, t][:, tokens], ACT.Sigmoid)
+                nc.vector.scalar_tensor_tensor(
+                    gated[:, :, HALF // 2 * h : HALF // 2 * (h + 1)].rearrange("p d v -> p v d"),
+                    sums[0, t][:, tokens].rearrange("p (v d) -> p v d", d=2),
+                    size[:, t : t + 1],
+                    sig[:].rearrange("p (v d) -> p v d", d=2),
+                    ALU.mult,
+                    ALU.mult,
+                )
+            nc.vector.tensor_tensor(lv1[t][:, :V], gated[:, 0, :], gated[:, 1, :], ALU.add)
             if t > 0:
                 nc.scalar.activation(st_sized[t][:], st_rest[:, t - 1, :], ACT.Copy, scale=size[:, t : t + 1])
 
-        hid = [held([P, LAST_CHUNK, PACK], BF16, "hid%d" % c) for c in range(U // LAST_CHUNK)]
-        lv2, lw = [], []
-
         def level_two(t):
-            lv2.append(held([P, U], F32, "lv2_%d" % t))
+            lv2[t] = held([P, U], F32, "lv2_%d" % t)
             for h in range(2):
+                columns = slice(HALF * h, HALF * (h + 1))
                 nc.vector.tensor_tensor(
-                    lv2[t][:, 256 * h : 256 * (h + 1)],
-                    lv1[t][:].indirect(m1_t[:, 16 * h : 16 * (h + 1)]),
-                    st_sized[t][:, 256 * h : 256 * (h + 1)],
+                    lv2[t][:, columns],
+                    lv1[t][:].indirect(entries(m1_t, HALF * h, HALF)),
+                    st_sized[t][:, columns],
                     ALU.add,
                 )
-            lw.append(held([P, U], BF16, "lw_%d" % t))
+            lw[t] = held([P, U], BF16, "lw_%d" % t)
             nc.vector.tensor_tensor(lw[t][:], lv2[t][:], lam_t[:, t, :], ALU.mult)
 
-        def read_other(t, j0, width):
-            other = ring.tile([P, width], BF16, name="other%d" % width)
-            nc.vector.tensor_copy(other[:], lv2[t][:].indirect(m2_t[:, j0 // 16 : (j0 + width) // 16]))
-            larger = ring.tile([P, width], BF16, name="larger%d" % width)
-            nc.vector.tensor_tensor(larger[:], other[:], lw[t][:, j0 : j0 + width], ALU.max)
-            for c in range(j0 // LAST_CHUNK, (j0 + width) // LAST_CHUNK):
+        def read_other(t, first, width):
+            other = held([P, width], BF16, "other%d_%d" % (t, first))
+            nc.vector.tensor_copy(other[:], lv2[t][:].indirect(entries(m2_t, first, width)))
+            larger = held([P, width], BF16, "larger%d_%d" % (t, first))
+            nc.vector.tensor_tensor(larger[:], other[:], lw[t][:, first : first + width], ALU.max)
+            for c in range(first // CHUNK, (first + width) // CHUNK):
                 nc.scalar.activation(
                     hid[c][:, :, t],
-                    larger[:, c * LAST_CHUNK - j0 : (c + 1) * LAST_CHUNK - j0],
+                    larger[:, c * CHUNK - first : (c + 1) * CHUNK - first],
                     ACT.Copy,
                     scale=sign[:, t : t + 1],
                 )
 
         def project(c):
-            codes = held([P, LAST_CHUNK], U32, "codes%d" % c)
-            plane = held([P, LAST_CHUNK], U8, "plane%d" % c)
+            codes = held([P, CHUNK], U32, "codes%d" % c)
+            scales = held([P, CHUNK], U8, "scales%d" % c)
             nc.vector.quantize_mx(
-                out=codes[:].bitcast(FP8X4), scales=plane[:], in_=hid[c][:].rearrange("p j t -> p (j t)")
+                out=codes[:].bitcast(FP8X4), scales=scales[:], in_=hid[c][:].rearrange("p j t -> p (j t)")
             )
-            acc = bank((2, 3, 6, 7)[c], [P, 2, LAST_CHUNK], "acc%d" % c)
-            for a in range(2):
+            projected = bank(4 + c, [P, N // P, CHUNK], "projected%d" % c)
+            for a in range(N // P):
                 nc.tensor.matmul_mx(
-                    out=acc[:, a, :],
+                    out=projected[:, a, :],
                     lhsT=w3w[:, 2 * P * a : 2 * P * (a + 1)].bitcast(FP4X4),
-                    lhsT_scale=w3_plane[:, P * a : P * (a + 1)],
+                    lhsT_scale=w3s[:, P * a : P * (a + 1)],
                     rhs=codes[:].bitcast(FP8X4),
-                    rhs_scale=plane[:],
+                    rhs_scale=scales[:],
                     start=True,
                     stop=True,
                 )
-            result = held([P, 2, LAST_CHUNK], F32, "result%d" % c)
-            nc.vector.tensor_copy(result[:], acc[:])
-            nc.sync.dma_start(
-                out.rearrange("(a p) j -> p a j", p=P)[:, :, c * LAST_CHUNK : (c + 1) * LAST_CHUNK], result[:]
-            )
+            result = held([P, N // P, CHUNK], F32, "result%d" % c)
+            nc.vector.tensor_copy(result[:], projected[:])
+            nc.sync.dma_start(out.rearrange("(a p) j -> p a j", p=P)[:, :, c * CHUNK : (c + 1) * CHUNK], result[:])
 
+        level_one(0)
+        level_one(1)
         level_two(0)
-        for t in range(PACK - 1):
+        for t in range(SLOTS - 1):
+            if t + 2 < SLOTS:
+                level_one(t + 2)
             level_two(t + 1)
             for h in range(2):
-                read_other(t, 256 * h, 256)
-        for c in range(U // LAST_CHUNK):
-            read_other(PACK - 1, c * LAST_CHUNK, LAST_CHUNK)
-        for c in range(U // LAST_CHUNK):
+                read_other(t, HALF * h, HALF)
+        for c in range(CHUNKS):
+            read_other(SLOTS - 1, c * CHUNK, CHUNK)
+        for c in range(CHUNKS):
             project(c)

@@ -51,12 +51,13 @@ def tile_picked_yfenw_max_p_kernel(
         zeros = [held([P, SPARE], F32, "xw%d" % o) for o in range(PASSES)]
         for o in range(PASSES):
             nc.vector.memset(zeros[o][:], 0.0)
-        nc.vector.memset(xs_window[:, : T // 2].bitcast(I32), 0)
-        nc.gpsimd.memset(xs_window[:, T // 2 :].bitcast(I32), 0)
-        nc.gpsimd.memset(ws_loaded[0][:].rearrange("p o c -> p (o c)").bitcast(I32), 0)
-        nc.vector.memset(ws_loaded[1][:].rearrange("p o c -> p (o c)").bitcast(I32), 0)
-        for t in range(SLOTS):
-            nc.vector.tensor_copy(lv1[t][:, V:], zeros[t // 2][:])
+        nc.vector.memset(xs_window[:].bitcast(I32), 0)
+        for t in range(2):
+            nc.vector.tensor_copy(lv1[t][:, V:], zeros[0][:])
+        for g in (1, 0):
+            nc.vector.memset(ws_loaded[g][:].rearrange("p o c -> p (o c)").bitcast(I32), 0)
+        for t in range(2, SLOTS):
+            nc.vector.tensor_copy(lv1[t][:, V:], zeros[1][:])
         nc.vector.memset(xs1[:].bitcast(I32), 0)
 
         def load_weight_scales(queue, g, q):
@@ -179,7 +180,7 @@ def tile_picked_yfenw_max_p_kernel(
                     ALU.add,
                 )
             lw[t] = held([P, U], BF16, "lw_%d" % t)
-            nc.vector.tensor_tensor(lw[t][:], lv2[t][:], lam_t[:, t, :], ALU.mult)
+            nc.gpsimd.tensor_tensor(lw[t][:], lv2[t][:], lam_t[:, t, :], ALU.mult)
 
         def read_other(t, first, width):
             other = held([P, width], BF16, "other%d_%d" % (t, first))

from contextlib import ExitStack

import concourse.mybir as mybir

K, T, S, H, V, U, N = 1024, 2048, 512, 512, 256, 512, 256
FLOPS = 2 * (2 * K * H * S + H * N * U)

F32 = mybir.dt.float32
BF16 = mybir.dt.bfloat16
I32 = mybir.dt.int32
U32 = mybir.dt.uint32
U16 = mybir.dt.uint16
U8 = mybir.dt.uint8
FP8X4 = mybir.dt.float8_e4m3fn_x4
FP4X4 = mybir.dt.float4_e2m1fn_x4
ALU = mybir.AluOpType
ACT = mybir.ActivationFunctionType

P = 128
SLOTS = 4
PASSES = K // (P * SLOTS)
QUADRANTS = 4
HALF = 256
SPARE = 16
CHUNK = 128
CHUNKS = U // CHUNK


def tile_picked_yfenw_max_p_kernel(
    tc, x_words, x_scales, w1_words, w1_scales, w2_words, w2_scales, st, lam, unit, w3_words, w3_scales, offs, m1, m2, out
):
    nc = tc.nc
    with ExitStack() as ctx:
        lists = ctx.enter_context(tc.tile_pool(name="lists", bufs=1))
        keep = ctx.enter_context(tc.tile_pool(name="keep", bufs=1))
        psum = ctx.enter_context(tc.psum_pool(name="psum", bufs=1))

        def held(shape, dtype, name, after=None):
            return keep.tile(shape, dtype, name=name, tag=after or name, align_bytes=64)

        def bank(index, shape, name):
            return psum.tile(shape, F32, name=name, tag="bank%d" % index)

        def entries(offsets, first, count):
            return offsets[:, first // 16 : (first + count) // 16]

        xs_window = held([P, T], U8, "xs_window")
        xs1 = held([P, S], U8, "xs1")
        ws_loaded = [held([P, PASSES, H], U8, "ws_loaded%d" % g) for g in range(2)]
        lv1 = [held([P, V + SPARE], F32, "lv1_%d" % t) for t in range(SLOTS)]
        zeros = [held([P, SPARE], F32, "xw%d" % o) for o in range(PASSES)]
        for o in range(PASSES):
            nc.vector.memset(zeros[o][:], 0.0)
        nc.vector.memset(xs_window[:].bitcast(I32), 0)
        for t in range(2):
            nc.vector.tensor_copy(lv1[t][:, V:], zeros[0][:])
        for g in (1, 0):
            nc.vector.memset(ws_loaded[g][:].rearrange("p o c -> p (o c)").bitcast(I32), 0)
        for t in range(2, SLOTS):
            nc.vector.tensor_copy(lv1[t][:, V:], zeros[1][:])
        nc.vector.memset(xs1[:].bitcast(I32), 0)

        def load_weight_scales(queue, g, q):
            queue.dma_start(
                ws_loaded[g][32 * q : 32 * q + 4, :, :].bitcast(I32),
                (w1_scales, w2_scales)[g][:, 4 * q : 4 * q + 4, :].rearrange("o r c -> r o c").bitcast(I32),
            )

        offs_t = lists.tile([P, S // 16], U16, name="offs_t")
        m1_t = lists.tile([P, U // 16], U16, name="m1_t")
        m2_t = lists.tile([P, U // 16], U16, name="m2_t")
        xw = [held([P, T], I32, "xw_table%d" % o, after="xw%d" % o) for o in range(PASSES)]
        ww_loaded = [held([P, PASSES, 2 * H], U8, "ww_loaded%d" % g) for g in range(2)]
        nc.sync.dma_start(offs_t[:], offs)
        nc.sync.dma_start(ww_loaded[1][:].bitcast(I32), w2_words.rearrange("o p c -> p o c").bitcast(I32))
        nc.sync.dma_start(ww_loaded[0][:].bitcast(I32), w1_words.rearrange("o p c -> p o c").bitcast(I32))
        for r in range(4):
            nc.sync.dma_start(
                xs_window[r:P:16, :].bitcast(I32),
                x_scales.rearrange("o (q r) c -> r q o c", r=4)[r].bitcast(I32),
            )
        nc.sync.dma_start(xw[0][:], x_words[0].rearrange("p c r -> p (c r)").bitcast(I32))
        for q in range(QUADRANTS):
            load_weight_scales(nc.sync, 1, q)
        for q in range(QUADRANTS):
            load_weight_scales(nc.gpsimd if q < 2 else nc.sync, 0, q)
        nc.sync.dma_start(xw[1][:], x_words[1].rearrange("p c r -> p (c r)").bitcast(I32))
        nc.sync.dma_start(m1_t[:], m1)
        nc.sync.dma_start(m2_t[:], m2)

        xs0 = held([P, S], U8, "xs0")
        nc.vector.tensor_copy(xs0[:], xs_window[:].indirect(offs_t[:]))
        for q in range(QUADRANTS):
            nc.sync.dma_start(xs1[32 * q : 32 * q + 4, :].bitcast(I32), xs0[32 * q + 16 : 32 * q + 20, :].bitcast(I32))
        xs = [xs0, xs1]
        st_rows = st.rearrange("(p t) j -> p t j", t=SLOTS)
        st_first = held([P, U + SLOTS], F32, "st_first", after="xs_window")
        unit_t = st_first[:, U:]
        nc.sync.dma_start(unit_t, unit.rearrange("(p t) one -> p (t one)", t=SLOTS))
        nc.sync.dma_start(st_first[:, :U], st_rows[:, 0, :])

        picked = [held([P, S], U32, "picked%d" % o) for o in range(PASSES)]
        for o in range(PASSES):
            nc.vector.tensor_copy(picked[o][:], xw[o][:].bitcast(U32).indirect(offs_t[:]))
        st_rest = held([P, SLOTS - 1, U], F32, "st_rest", after="xw0")
        nc.sync.dma_start(st_rest[:], st_rows[:, 1:, :])

        ww, ws = {}, {}
        for o in range(PASSES):
            for g in (1, 0):
                ww[g, o] = held([P, SLOTS, P, 2], U8, "ww%d%d" % (g, o))
                ws[g, o] = held([P, SLOTS, P], U8, "ws%d%d" % (g, o))
                nc.vector.tensor_copy(ws[g, o][:], ws_loaded[g][:, o, :].rearrange("p (m t) -> p t m", t=SLOTS))
                nc.vector.tensor_copy(ww[g, o][:], ww_loaded[g][:, o, :].rearrange("p (m t b) -> p t m b", t=SLOTS, b=2))

        late = held([P, SLOTS * U + 24], F32, "late", after="xw1")
        lam_t = late[:, : SLOTS * U].rearrange("p (t j) -> p t j", t=SLOTS)
        size = late[:, SLOTS * U : SLOTS * U + SLOTS]
        twice_plus = late[:, SLOTS * U + 8 : SLOTS * U + 8 + SLOTS]
        sign = late[:, SLOTS * U + 16 : SLOTS * U + 16 + SLOTS]
        st_sized = [held([P, U], F32, "st_sized%d" % t) for t in range(SLOTS)]
        nc.vector.scalar_tensor_tensor(size, unit_t, -1.0, unit_t, ALU.mult, ALU.max)
        nc.vector.tensor_scalar(twice_plus, unit_t, 0.0, 2.0, ALU.is_ge, ALU.mult)
        nc.vector.tensor_scalar(st_sized[0][:], st_first[:, :U], size[:, 0:1], None, ALU.mult)
        nc.vector.tensor_scalar(sign, twice_plus, -1.0, None, ALU.add)
        nc.sync.dma_start(late[:, : SLOTS * U], lam.rearrange("(p t) j -> p (t j)", t=SLOTS))
        w3w = held([P, 2 * N], U8, "w3w", after="ws_loaded1")
        w3s = held([P, N], U8, "w3s", after="ws_loaded0")
        nc.vector.memset(w3s[:].bitcast(I32), 0)
        nc.sync.dma_start(w3w[:].bitcast(I32), w3_words[0].bitcast(I32))
        for q in range(QUADRANTS):
            nc.sync.dma_start(w3s[32 * q : 32 * q + 4, :].bitcast(I32), w3_scales[0, 4 * q : 4 * q + 4, :].bitcast(I32))

        sums = {}

        def products(t):
            for g in (1, 0):
                sums[g, t] = bank(2 * (t % 2) + g, [P, S], "sums%d%d" % (g, t))
                for o in range(PASSES):
                    nc.tensor.matmul_mx(
                        out=sums[g, t][:],
                        lhsT=ww[g, o][:, t, :, :].rearrange("p m b -> p (m b)").bitcast(FP4X4),
                        lhsT_scale=ws[g, o][:, t, :],
                        rhs=picked[o][:].bitcast(FP8X4),
                        rhs_scale=xs[o][:],
                        start=(o == 0),
                        stop=(o == PASSES - 1),
                    )

        hid = [held([P, CHUNK, SLOTS], BF16, "hid%d" % c) for c in range(CHUNKS)]
        lv2, lw = {}, {}

        def level_one(t):
            products(t)
            gated = held([P, 2, V], F32, "gated%d" % t)
            for h in range(2):
                tokens = slice(HALF * h, HALF * (h + 1))
                sig = held([P, HALF], F32, "sig%d%d" % (t, h))
                nc.scalar.activation(sig[:], sums[1, t][:, tokens], ACT.Sigmoid)
                nc.vector.scalar_tensor_tensor(
                    gated[:, :, HALF // 2 * h : HALF // 2 * (h + 1)].rearrange("p d v -> p v d"),
                    sums[0, t][:, tokens].rearrange("p (v d) -> p v d", d=2),
                    size[:, t : t + 1],
                    sig[:].rearrange("p (v d) -> p v d", d=2),
                    ALU.mult,
                    ALU.mult,
                )
            nc.vector.tensor_tensor(lv1[t][:, :V], gated[:, 0, :], gated[:, 1, :], ALU.add)
            if t > 0:
                nc.scalar.activation(st_sized[t][:], st_rest[:, t - 1, :], ACT.Copy, scale=size[:, t : t + 1])

        def level_two(t):
            lv2[t] = held([P, U], F32, "lv2_%d" % t)
            for h in range(2):
                columns = slice(HALF * h, HALF * (h + 1))
                nc.vector.tensor_tensor(
                    lv2[t][:, columns],
                    lv1[t][:].indirect(entries(m1_t, HALF * h, HALF)),
                    st_sized[t][:, columns],
                    ALU.add,
                )
            lw[t] = held([P, U], BF16, "lw_%d" % t)
            nc.gpsimd.tensor_tensor(lw[t][:], lv2[t][:], lam_t[:, t, :], ALU.mult)

        def read_other(t, first, width):
            other = held([P, width], BF16, "other%d_%d" % (t, first))
            nc.vector.tensor_copy(other[:], lv2[t][:].indirect(entries(m2_t, first, width)))
            larger = held([P, width], BF16, "larger%d_%d" % (t, first))
            nc.vector.tensor_tensor(larger[:], other[:], lw[t][:, first : first + width], ALU.max)
            for c in range(first // CHUNK, (first + width) // CHUNK):
                nc.scalar.activation(
                    hid[c][:, :, t],
                    larger[:, c * CHUNK - first : (c + 1) * CHUNK - first],
                    ACT.Copy,
                    scale=sign[:, t : t + 1],
                )

        def project(c):
            codes = held([P, CHUNK], U32, "codes%d" % c)
            scales = held([P, CHUNK], U8, "scales%d" % c)
            nc.vector.quantize_mx(
                out=codes[:].bitcast(FP8X4), scales=scales[:], in_=hid[c][:].rearrange("p j t -> p (j t)")
            )
            projected = bank(4 + c, [P, N // P, CHUNK], "projected%d" % c)
            for a in range(N // P):
                nc.tensor.matmul_mx(
                    out=projected[:, a, :],
                    lhsT=w3w[:, 2 * P * a : 2 * P * (a + 1)].bitcast(FP4X4),
                    lhsT_scale=w3s[:, P * a : P * (a + 1)],
                    rhs=codes[:].bitcast(FP8X4),
                    rhs_scale=scales[:],
                    start=True,
                    stop=True,
                )
            result = held([P, N // P, CHUNK], F32, "result%d" % c)
            nc.vector.tensor_copy(result[:], projected[:])
            nc.sync.dma_start(out.rearrange("(a p) j -> p a j", p=P)[:, :, c * CHUNK : (c + 1) * CHUNK], result[:])

        level_one(0)
        level_one(1)
        level_two(0)
        for t in range(SLOTS - 1):
            if t + 2 < SLOTS:
                level_one(t + 2)
            level_two(t + 1)
            for h in range(2):
                read_other(t, HALF * h, HALF)
        for c in range(CHUNKS):
            read_other(SLOTS - 1, c * CHUNK, CHUNK)
        for c in range(CHUNKS):
            project(c)
